import numpy as np
import ml_dtypes


def mxq(x, axis, fmt="e4m3"):
    dtype, down = {"e4m3": (ml_dtypes.float8_e4m3fn, 7), "e5m2": (ml_dtypes.float8_e5m2, 14)}[fmt]
    v = np.moveaxis(np.asarray(x, np.float32).astype(ml_dtypes.bfloat16).astype(np.float64), axis, -1)
    blocks = v.reshape(v.shape[:-1] + (-1, 32))
    amax = np.abs(blocks).max(-1, keepdims=True)
    byte = np.maximum(np.where(amax > 0, np.frexp(amax)[1] - 1 + 127, 0) - down, 1)
    scale = np.exp2(byte - 127.0)
    codes = (blocks / scale).astype(np.float32).astype(dtype).astype(np.float64)
    return np.moveaxis((codes * scale).reshape(v.shape), -1, axis)


WIDE = False


def mx_kscale(k):
    if not WIDE:
        return np.ones(k)
    levels = np.array([10, -10, 5, -5, 0])
    if k % 512:
        return np.exp2(np.random.permutation(np.resize(levels, k // 32))).repeat(32)
    a = np.empty((k // 512, 16))
    for p in range(k // 512):
        a[p, :8] = np.random.permutation(np.resize(levels, 8))
        for g in range(8):
            far = levels[np.abs(levels - a[p, g]) >= 10]
            a[p, g + 8] = far[np.random.randint(len(far))]
    return np.exp2(a.ravel()).repeat(32)


def f64(x):
    return np.asarray(x).astype(np.float64)


def striped(idx):
    return np.tile(idx.reshape(-1, 16).T, (8, 1)).astype(np.uint16)


def unstriped(offs):
    return offs[:16].T.reshape(-1).astype(np.int64)


E2M1 = np.array([0.0, 0.5, 1.0, 1.5, 2.0, 3.0, 4.0, 6.0, -0.0, -0.5, -1.0, -1.5, -2.0, -3.0, -4.0, -6.0])


def pack_fp4(w):
    k, n = w.shape
    w = f64(np.asarray(w, np.float32).astype(ml_dtypes.bfloat16)).reshape(k // 32, 32, n)
    amax = np.abs(w).max(1)
    mant, ex = np.frexp(amax / 6.0)
    byte = np.clip(np.where(amax > 0, np.where(mant > 0.5, ex, ex - 1) + 127, 1), 1, 254)
    scaled = (w * np.exp2(127.0 - byte)[:, None, :]).reshape(k, n).astype(np.float32)
    c = np.ascontiguousarray(scaled.reshape(k // 512, 128, 4, n).transpose(0, 1, 3, 2)).astype(ml_dtypes.float4_e2m1fn).view(np.uint8) & 0xF
    words = (c[..., 0::2] | (c[..., 1::2] << 4)).reshape(k // 512, 128, 2 * n)
    return np.ascontiguousarray(words), np.ascontiguousarray(byte.astype(np.uint8).reshape(k // 512, 16, n))


def unpack_fp4(words, scales):
    g, _, n = scales.shape
    words = np.ascontiguousarray(words).reshape(g, 128, n, 2)
    nib = np.empty((g, 128, n, 4), np.uint8)
    nib[..., 0::2] = words & 0xF
    nib[..., 1::2] = words >> 4
    vals = E2M1[nib] * np.repeat(np.exp2(scales.astype(np.float64) - 127.0), 8, axis=1)[..., None]
    return vals.transpose(0, 1, 3, 2).reshape(g * 512, n)


def silu(v):
    return v / (1.0 + np.exp(-np.maximum(v, -700.0)))


K, T, S, V, N = 1024, 2048, 512, 256, 256


def setup_inputs():
    n = np.random.standard_normal
    s = mx_kscale(K)[:, None]
    packed_xT = pack_fp4(n((K, T)) * s)
    return {
        "x_words": packed_xT[0],
        "x_scales": packed_xT[1],
        "w1": (n((K, N)) / np.sqrt(K) / s).astype(np.float32),
        "w2": (n((K, N)) / np.sqrt(K) / s).astype(np.float32),
        "w3": (n((K, N)) / np.sqrt(K) / s).astype(np.float32),
        "offs": striped(np.random.permutation(T)[:S]),
        "cen": striped(np.random.permutation(S)[:V]),
        "pos1": striped(np.random.permutation(S)[:V]),
        "pos2": striped(np.random.permutation(S)[:V]),
        "pos3": striped(np.random.permutation(S)[:V]),
    }


def reference(x_words, x_scales, w1, w2, w3, offs, cen, pos1, pos2, pos3):
    xq = unpack_fp4(x_words, x_scales)[:, unstriped(offs)]
    h = mxq(f64(w3), 0, "e4m3").T @ xq
    g = mxq(f64(w1), 0, "e4m3").T @ xq
    gc = g[:, unstriped(cen)]
    s = mxq(f64(w2), 0, "e4m3").T @ xq
    sc = s[:, unstriped(cen)]
    return silu(h[:, unstriped(pos1)] * gc + sc) + silu(h[:, unstriped(pos2)] * gc + sc) + silu(h[:, unstriped(pos3)] * gc + sc)

@@ -1,0 +1,187 @@
+from contextlib import ExitStack
+
+import concourse.mybir as mybir
+from concourse.masks import make_identity
+
+K, T, S, V, N = 1024, 2048, 512, 256, 256
+FLOPS = 3 * 2 * K * N * S
+
+F32 = mybir.dt.float32
+BF16 = mybir.dt.bfloat16
+I32 = mybir.dt.int32
+U32 = mybir.dt.uint32
+U16 = mybir.dt.uint16
+U8 = mybir.dt.uint8
+FP8X4 = mybir.dt.float8_e4m3fn_x4
+FP4X4 = mybir.dt.float4_e2m1fn_x4
+MULT = mybir.AluOpType.mult
+ADD = mybir.AluOpType.add
+SILU = mybir.ActivationFunctionType.Silu
+
+P = 128
+PACK = 4
+K_PASS = P * PACK
+PASSES = K // K_PASS
+BLOCKS = N // P
+HALVES = V // P
+
+
+def tile_picked_filmg_silu_p_kernel(
+    tc, x_words, x_scales, w1, w2, w3, offs, cen, pos1, pos2, pos3, out
+):
+    nc = tc.nc
+    with ExitStack() as ctx:
+        keep = ctx.enter_context(tc.tile_pool(name="keep", bufs=1))
+        psum = ctx.enter_context(tc.psum_pool(name="psum", bufs=1))
+
+        def load_list(name, src):
+            tile = keep.tile(list(src.shape), U16, name=name)
+            nc.sync.dma_start(tile[:], src)
+            return tile
+
+        def load_words(z):
+            tile = keep.tile([P, T], U16, name="xw%d" % z, align_bytes=64)
+            nc.sync.dma_start(tile[:].bitcast(I32), x_words[z].bitcast(I32))
+            return tile
+
+        def load_weight(name, w, z):
+            raw = keep.tile([P, PACK, N], F32, name="raw_%s%d" % (name, z), align_bytes=64)
+            nc.sync.dma_start(raw[:], w[z * K_PASS : (z + 1) * K_PASS, :].rearrange("(p j) n -> p j n", j=PACK))
+            return raw
+
+        def interleave(name, raw, z, on_vector):
+            grouped = keep.tile([P, N, PACK], BF16, name="grp_%s%d" % (name, z), align_bytes=64)
+            dst = grouped[:].rearrange("p (c i) t -> p c t i", i=4)
+            src = raw[:].rearrange("p t (c i) -> p c t i", i=4)
+            if on_vector:
+                nc.vector.tensor_copy(dst, src)
+            else:
+                nc.scalar.copy(dst, src)
+            return grouped
+
+        def quantize(name, grouped, z):
+            codes = keep.tile([P, N], U32, name="codes_%s%d" % (name, z), align_bytes=64)
+            plane = keep.tile([P, N], U8, name="plane_%s%d" % (name, z), align_bytes=64)
+            nc.vector.quantize_mx(
+                out=codes[:].bitcast(FP8X4), scales=plane[:], in_=grouped[:].rearrange("p n t -> p (n t)")
+            )
+            return codes, plane
+
+        def gather(name, window, offsets, dtype):
+            picked = keep.tile([P, 16 * offsets.shape[1]], dtype, name=name, align_bytes=64)
+            nc.vector.tensor_copy(picked[:], window.indirect(offsets[:]))
+            return picked
+
+        warm = keep.tile([P, 1], F32, name="warm")
+        nc.gpsimd.memset(warm[:], 0.0)
+        warm2 = keep.tile([P, 1], F32, name="warm2")
+        nc.scalar.activation(warm2[:], warm[:], SILU)
+
+        xs = keep.tile([P, PASSES, T], U8, name="xs", align_bytes=64)
+        nc.vector.memset(xs[:].rearrange("p z c -> p (z c)").bitcast(I32), 0)
+        offs_t = load_list("offs_t", offs)
+        xw = [load_words(0)]
+        for q in range(4):
+            nc.sync.dma_start(
+                xs[32 * q : 32 * q + 4, :, :].bitcast(I32),
+                x_scales[:, 4 * q : 4 * q + 4, :].rearrange("z j c -> j z c").bitcast(I32),
+            )
+        raws = {}
+        raws["g", 0] = load_weight("g", w1, 0)
+        xw.append(load_words(1))
+        raws["g", 1] = load_weight("g", w1, 1)
+        cen_t = load_list("cen_t", cen)
+        raws["h", 0] = load_weight("h", w3, 0)
+        raws["h", 1] = load_weight("h", w3, 1)
+        pos_t = [load_list("pos1_t", pos1), load_list("pos2_t", pos2), load_list("pos3_t", pos3)]
+        raws["s", 0] = load_weight("s", w2, 0)
+        raws["s", 1] = load_weight("s", w2, 1)
+
+        ident = keep.tile([P, P], F32, name="ident")
+        make_identity(nc, ident[:])
+
+        xg, xsg = [], []
+        banks = {}
+        rows = {}
+
+        def product_pass(name, z, tags, on_vector):
+            codes, plane = quantize(name, interleave(name, raws[name, z], z, on_vector), z)
+            for b in range(BLOCKS):
+                if z == 0:
+                    banks[name, b] = psum.tile([P, S], F32, name="acc_%s%d" % (name, b), tag=tags[b])
+                cols = slice(b * P, (b + 1) * P)
+                nc.tensor.matmul_mx(
+                    out=banks[name, b][:],
+                    lhsT=codes[:, cols].bitcast(FP8X4),
+                    lhsT_scale=plane[:, cols],
+                    rhs=xg[z][:].bitcast(FP4X4),
+                    rhs_scale=xsg[z][:],
+                    start=(z == 0),
+                    stop=(z == PASSES - 1),
+                )
+
+        def leave(name, b):
+            rows[name, b] = keep.tile([P, S], F32, name="row_%s%d" % (name, b), align_bytes=64)
+            nc.scalar.copy(rows[name, b][:], banks[name, b][:])
+
+        for z in range(PASSES):
+            xg.append(gather("xg%d" % z, xw[z][:], offs_t, U16))
+            xsg.append(gather("xsg%d" % z, xs[:, z, :], offs_t, U8))
+            product_pass("g", z, ["b0", "b1"], False)
+        product_pass("h", 0, ["b2", "b3"], False)
+        leave("g", 0)
+        product_pass("h", 1, ["b2", "b3"], True)
+        leave("g", 1)
+        gc = [gather("gc%d" % b, rows["g", b][:], cen_t, F32) for b in range(BLOCKS)]
+        leave("h", 0)
+        product_pass("s", 0, ["b0", "b1"], False)
+        leave("h", 1)
+        product_pass("s", 1, ["b0", "b1"], False)
+        leave("s", 0)
+        leave("s", 1)
+
+        prod = {}
+
+        def products(b):
+            for d in range(3):
+                prod[b, d] = keep.tile([P, V], F32, name="prod%d_%d" % (b, d), align_bytes=64)
+                nc.vector.tensor_tensor(prod[b, d][:], rows["h", b][:].indirect(pos_t[d][:]), gc[b][:], MULT)
+
+        products(0)
+        sc0 = gather("sc0", rows["s", 0][:], cen_t, F32)
+        products(1)
+        sc1 = gather("sc1", rows["s", 1][:], cen_t, F32)
+
+        total = psum.tile([P, V], F32, name="total", tag="b7")
+        acts = []
+        for d in range(3):
+            u = psum.tile([P, HALVES, P], F32, name="u%d" % d, tag="b%d" % (4 + d))
+            for hv in range(HALVES):
+                cols = slice(hv * P, (hv + 1) * P)
+                nc.tensor.matmul(u[:, hv, :], prod[0, d][:, cols], ident[:], is_transpose=True, start=True, stop=False)
+                nc.tensor.matmul(u[:, hv, :], sc0[:, cols], ident[:], is_transpose=True, start=False, stop=True)
+            act = keep.tile([P, HALVES, P], F32, name="act%d" % d, align_bytes=64)
+            nc.scalar.activation(act[:], u[:], SILU)
+            acts.append(act)
+        for hv in range(HALVES):
+            for d in range(3):
+                nc.tensor.matmul(
+                    total[:, hv * P : (hv + 1) * P], acts[d][:, hv, :], ident[:],
+                    is_transpose=True, start=(d == 0), stop=(d == 2),
+                )
+        res0 = keep.tile([P, V], F32, name="res0", align_bytes=64)
+        nc.scalar.copy(res0[:], total[:])
+        nc.sync.dma_start(out[0:P, :], res0[:])
+
+        acts1 = []
+        for d in range(3):
+            u1 = keep.tile([P, V], F32, name="v%d" % d, align_bytes=64)
+            nc.vector.tensor_tensor(u1[:], prod[1, d][:], sc1[:], ADD)
+            act1 = keep.tile([P, V], F32, name="actv%d" % d, align_bytes=64)
+            nc.scalar.activation(act1[:], u1[:], SILU)
+            acts1.append(act1)
+        part = keep.tile([P, V], F32, name="part", align_bytes=64)
+        nc.vector.tensor_tensor(part[:], acts1[0][:], acts1[1][:], ADD)
+        res1 = keep.tile([P, V], F32, name="res1", align_bytes=64)
+        nc.vector.tensor_tensor(res1[:], part[:], acts1[2][:], ADD)
+        nc.sync.dma_start(out[P : 2 * P, :], res1[:])

@@ -22,8 +22,8 @@ P = 128
 PACK = 4
 K_PASS = P * PACK
 PASSES = K // K_PASS
-BLOCKS = N // P
 HALVES = V // P
+BOTH = (0, 1)
 
 
 def tile_picked_filmg_silu_p_kernel(
@@ -34,82 +34,94 @@ def tile_picked_filmg_silu_p_kernel(
         keep = ctx.enter_context(tc.tile_pool(name="keep", bufs=1))
         psum = ctx.enter_context(tc.psum_pool(name="psum", bufs=1))
 
+        def sbuf(name, shape, dtype, after=None):
+            return keep.tile(shape, dtype, name=name, tag=after or name, align_bytes=64)
+
         def load_list(name, src):
             tile = keep.tile(list(src.shape), U16, name=name)
             nc.sync.dma_start(tile[:], src)
             return tile
 
         def load_words(z):
-            tile = keep.tile([P, T], U16, name="xw%d" % z, align_bytes=64)
+            tile = sbuf("xw%d" % z, [P, T], U16)
             nc.sync.dma_start(tile[:].bitcast(I32), x_words[z].bitcast(I32))
             return tile
 
-        def load_weight(name, w, z):
-            raw = keep.tile([P, PACK, N], F32, name="raw_%s%d" % (name, z), align_bytes=64)
-            nc.sync.dma_start(raw[:], w[z * K_PASS : (z + 1) * K_PASS, :].rearrange("(p j) n -> p j n", j=PACK))
-            return raw
+        raws = {}
 
-        def interleave(name, raw, z, on_vector):
-            grouped = keep.tile([P, N, PACK], BF16, name="grp_%s%d" % (name, z), align_bytes=64)
-            dst = grouped[:].rearrange("p (c i) t -> p c t i", i=4)
-            src = raw[:].rearrange("p t (c i) -> p c t i", i=4)
-            if on_vector:
-                nc.vector.tensor_copy(dst, src)
-            else:
-                nc.scalar.copy(dst, src)
-            return grouped
+        def load_weight(name, w, z, blocks):
+            raw = sbuf("raw_%s%d%d" % (name, z, blocks[0]), [P, PACK, P * len(blocks)], F32)
+            rows_k = w[z * K_PASS : (z + 1) * K_PASS, blocks[0] * P : (blocks[-1] + 1) * P]
+            nc.sync.dma_start(raw[:], rows_k.rearrange("(p j) n -> p j n", j=PACK))
+            for i, b in enumerate(blocks):
+                raws[name, z, b] = (raw, i * P)
 
-        def quantize(name, grouped, z):
-            codes = keep.tile([P, N], U32, name="codes_%s%d" % (name, z), align_bytes=64)
-            plane = keep.tile([P, N], U8, name="plane_%s%d" % (name, z), align_bytes=64)
-            nc.vector.quantize_mx(
-                out=codes[:].bitcast(FP8X4), scales=plane[:], in_=grouped[:].rearrange("p n t -> p (n t)")
-            )
-            return codes, plane
-
-        def gather(name, window, offsets, dtype):
-            picked = keep.tile([P, 16 * offsets.shape[1]], dtype, name=name, align_bytes=64)
-            nc.vector.tensor_copy(picked[:], window.indirect(offsets[:]))
+        def gather(name, window, offsets, dtype, after=None):
+            picked = sbuf(name, [P, 16 * offsets.shape[1]], dtype, after)
+            nc.vector.tensor_copy(picked[:], window[:].indirect(offsets[:]))
             return picked
 
-        warm = keep.tile([P, 1], F32, name="warm")
-        nc.gpsimd.memset(warm[:], 0.0)
-        warm2 = keep.tile([P, 1], F32, name="warm2")
-        nc.scalar.activation(warm2[:], warm[:], SILU)
+        warm_in = keep.tile([P, 1], F32, name="warm_in")
+        nc.gpsimd.memset(warm_in[:], 0.0)
+        warm_out = keep.tile([P, 1], F32, name="warm_out")
+        nc.scalar.activation(warm_out[:], warm_in[:], SILU)
 
-        xs = keep.tile([P, PASSES, T], U8, name="xs", align_bytes=64)
-        nc.vector.memset(xs[:].rearrange("p z c -> p (z c)").bitcast(I32), 0)
+        xs = sbuf("xs", [P, T], U8)
+        nc.gpsimd.memset(xs[:].bitcast(I32), 0)
+        xs_second = sbuf("xs_second", [P, S], U8)
+        nc.gpsimd.memset(xs_second[:].bitcast(I32), 0)
         offs_t = load_list("offs_t", offs)
         xw = [load_words(0)]
         for q in range(4):
-            nc.sync.dma_start(
-                xs[32 * q : 32 * q + 4, :, :].bitcast(I32),
-                x_scales[:, 4 * q : 4 * q + 4, :].rearrange("z j c -> j z c").bitcast(I32),
-            )
-        raws = {}
-        raws["g", 0] = load_weight("g", w1, 0)
+            nc.sync.dma_start(xs[32 * q : 32 * q + 8, :].bitcast(I32), x_scales[:, 4 * q : 4 * q + 4, :].bitcast(I32))
+        load_weight("g", w1, 0, BOTH)
         xw.append(load_words(1))
-        raws["g", 1] = load_weight("g", w1, 1)
+        load_weight("g", w1, 1, BOTH)
+        load_weight("s", w2, 0, BOTH)
+        xg = [gather("xg0", xw[0], offs_t, U16)]
+        xs_first = gather("xs_first", xs, offs_t, U8)
+        nc.sync.dma_start(xs_second[0:112, :].bitcast(I32), xs_first[4:116, :].bitcast(I32))
+        xsg = [xs_first, xs_second]
         cen_t = load_list("cen_t", cen)
-        raws["h", 0] = load_weight("h", w3, 0)
-        raws["h", 1] = load_weight("h", w3, 1)
+        load_weight("s", w2, 1, BOTH)
+        load_weight("h", w3, 0, (0,))
+        load_weight("h", w3, 1, (0,))
+        load_weight("h", w3, 0, (1,))
+        load_weight("h", w3, 1, (1,))
         pos_t = [load_list("pos1_t", pos1), load_list("pos2_t", pos2), load_list("pos3_t", pos3)]
-        raws["s", 0] = load_weight("s", w2, 0)
-        raws["s", 1] = load_weight("s", w2, 1)
 
         ident = keep.tile([P, P], F32, name="ident")
         make_identity(nc, ident[:])
 
-        xg, xsg = [], []
-        banks = {}
-        rows = {}
+        banks, rows, grouped = {}, {}, {}
+        bank_tag = {("g", 0): "b0", ("g", 1): "b1", ("s", 0): "b2", ("s", 1): "b3", ("h", 0): "b4", ("h", 1): "b5"}
 
-        def product_pass(name, z, tags, on_vector):
-            codes, plane = quantize(name, interleave(name, raws[name, z], z, on_vector), z)
-            for b in range(BLOCKS):
+        def cast(name, z, blocks, on_vector=False):
+            raw, first = raws[name, z, blocks[0]]
+            width = P * len(blocks)
+            tile = sbuf("grp_%s%d%d" % (name, z, blocks[0]), [P, width, PACK], BF16)
+            dst = tile[:].rearrange("p (c i) t -> p c t i", i=4)
+            src = raw[:, :, first : first + width].rearrange("p t (c i) -> p c t i", i=4)
+            if on_vector:
+                nc.vector.tensor_copy(dst, src)
+            else:
+                nc.scalar.copy(dst, src)
+            grouped[name, z, blocks[0]] = tile
+
+        def multiply(name, z, blocks):
+            label = "%s%d%d" % (name, z, blocks[0])
+            width = P * len(blocks)
+            codes = sbuf("codes_" + label, [P, width], U32)
+            plane = sbuf("plane_" + label, [P, width], U8)
+            nc.vector.quantize_mx(
+                out=codes[:].bitcast(FP8X4),
+                scales=plane[:],
+                in_=grouped[name, z, blocks[0]][:].rearrange("p n t -> p (n t)"),
+            )
+            for i, b in enumerate(blocks):
                 if z == 0:
-                    banks[name, b] = psum.tile([P, S], F32, name="acc_%s%d" % (name, b), tag=tags[b])
-                cols = slice(b * P, (b + 1) * P)
+                    banks[name, b] = psum.tile([P, S], F32, name="acc_%s%d" % (name, b), tag=bank_tag[name, b])
+                cols = slice(i * P, (i + 1) * P)
                 nc.tensor.matmul_mx(
                     out=banks[name, b][:],
                     lhsT=codes[:, cols].bitcast(FP8X4),
@@ -120,68 +132,92 @@ def tile_picked_filmg_silu_p_kernel(
                     stop=(z == PASSES - 1),
                 )
 
-        def leave(name, b):
-            rows[name, b] = keep.tile([P, S], F32, name="row_%s%d" % (name, b), align_bytes=64)
+        def leave(name, b, after=None):
+            rows[name, b] = sbuf("row_%s%d" % (name, b), [P, S], F32, after)
             nc.scalar.copy(rows[name, b][:], banks[name, b][:])
 
-        for z in range(PASSES):
-            xg.append(gather("xg%d" % z, xw[z][:], offs_t, U16))
-            xsg.append(gather("xsg%d" % z, xs[:, z, :], offs_t, U8))
-            product_pass("g", z, ["b0", "b1"], False)
-        product_pass("h", 0, ["b2", "b3"], False)
-        leave("g", 0)
-        product_pass("h", 1, ["b2", "b3"], True)
-        leave("g", 1)
-        gc = [gather("gc%d" % b, rows["g", b][:], cen_t, F32) for b in range(BLOCKS)]
-        leave("h", 0)
-        product_pass("s", 0, ["b0", "b1"], False)
-        leave("h", 1)
-        product_pass("s", 1, ["b0", "b1"], False)
-        leave("s", 0)
-        leave("s", 1)
+        def scaled(dst, b, d):
+            nc.vector.tensor_tensor(dst, rows["h", b][:].indirect(pos_t[d][:]), gc[b][:], MULT)
 
-        prod = {}
-
-        def products(b):
-            for d in range(3):
-                prod[b, d] = keep.tile([P, V], F32, name="prod%d_%d" % (b, d), align_bytes=64)
-                nc.vector.tensor_tensor(prod[b, d][:], rows["h", b][:].indirect(pos_t[d][:]), gc[b][:], MULT)
-
-        products(0)
-        sc0 = gather("sc0", rows["s", 0][:], cen_t, F32)
-        products(1)
-        sc1 = gather("sc1", rows["s", 1][:], cen_t, F32)
-
-        total = psum.tile([P, V], F32, name="total", tag="b7")
-        acts = []
-        for d in range(3):
-            u = psum.tile([P, HALVES, P], F32, name="u%d" % d, tag="b%d" % (4 + d))
+        def turn(bank, src, start, stop):
             for hv in range(HALVES):
                 cols = slice(hv * P, (hv + 1) * P)
-                nc.tensor.matmul(u[:, hv, :], prod[0, d][:, cols], ident[:], is_transpose=True, start=True, stop=False)
-                nc.tensor.matmul(u[:, hv, :], sc0[:, cols], ident[:], is_transpose=True, start=False, stop=True)
-            act = keep.tile([P, HALVES, P], F32, name="act%d" % d, align_bytes=64)
-            nc.scalar.activation(act[:], u[:], SILU)
-            acts.append(act)
-        for hv in range(HALVES):
-            for d in range(3):
                 nc.tensor.matmul(
-                    total[:, hv * P : (hv + 1) * P], acts[d][:, hv, :], ident[:],
-                    is_transpose=True, start=(d == 0), stop=(d == 2),
+                    bank[:, cols], src[:, cols], ident[:], is_transpose=True,
+                    start=(start and hv == 0), stop=(stop and hv == HALVES - 1),
                 )
-        res0 = keep.tile([P, V], F32, name="res0", align_bytes=64)
-        nc.scalar.copy(res0[:], total[:])
-        nc.sync.dma_start(out[0:P, :], res0[:])
 
-        acts1 = []
+        def silu(name, src):
+            act = sbuf(name, [P, V], F32)
+            nc.scalar.activation(act[:], src, SILU)
+            return act
+
+        cast("g", 0, BOTH)
+        multiply("g", 0, BOTH)
+        xg.append(gather("xg1", xw[1], offs_t, U16, "grp_g00"))
+        cast("g", 1, (0,))
+        cast("g", 1, (1,))
+        multiply("g", 1, (0,))
+        multiply("g", 1, (1,))
+        cast("s", 0, BOTH, True)
+        leave("g", 0)
+        multiply("s", 0, BOTH)
+        cast("s", 1, (0,))
+        cast("s", 1, (1,))
+        gc = [gather("gc0", rows["g", 0], cen_t, F32)]
+        cast("h", 0, (0,), True)
+        multiply("s", 1, (0,))
+        multiply("h", 0, (0,))
+        cast("h", 1, (0,), True)
+        multiply("h", 1, (0,))
+        multiply("s", 1, (1,))
+        leave("g", 1, "raw_s10")
+        leave("s", 0)
+        gc.append(gather("gc1", rows["g", 1], cen_t, F32, "grp_h10"))
+        cast("h", 0, (1,), True)
+        cast("h", 1, (1,))
+        leave("s", 1)
+        leave("h", 0)
+        sc = [gather("sc0", rows["s", 0], cen_t, F32)]
+        multiply("h", 0, (1,))
+        multiply("h", 1, (1,))
+        sc.append(gather("sc1", rows["s", 1], cen_t, F32))
+        prod0 = sbuf("prod0", [P, 3, V], F32, "row_s1")
         for d in range(3):
-            u1 = keep.tile([P, V], F32, name="v%d" % d, align_bytes=64)
-            nc.vector.tensor_tensor(u1[:], prod[1, d][:], sc1[:], ADD)
-            act1 = keep.tile([P, V], F32, name="actv%d" % d, align_bytes=64)
-            nc.scalar.activation(act1[:], u1[:], SILU)
-            acts1.append(act1)
-        part = keep.tile([P, V], F32, name="part", align_bytes=64)
-        nc.vector.tensor_tensor(part[:], acts1[0][:], acts1[1][:], ADD)
-        res1 = keep.tile([P, V], F32, name="res1", align_bytes=64)
-        nc.vector.tensor_tensor(res1[:], part[:], acts1[2][:], ADD)
+            scaled(prod0[:, d, :], 0, d)
+        leave("h", 1)
+        prod10 = sbuf("prod10", [P, V], F32)
+        scaled(prod10[:], 1, 0)
+        prod1 = sbuf("prod1", [P, 2, V], F32)
+        scaled(prod1[:, 0, :], 1, 1)
+        scaled(prod1[:, 1, :], 1, 2)
+
+        u = {}
+        for b, d, tag in ((0, 0, "b0"), (0, 1, "b1"), (0, 2, "b2"), (1, 0, "b3"), (1, 1, "b6")):
+            u[b, d] = psum.tile([P, V], F32, name="u%d%d" % (b, d), tag=tag)
+            turn(u[b, d], sc[b], True, False)
+        total0 = psum.tile([P, V], F32, name="total0", tag="b7")
+        turn(u[0, 0], prod0[:, 0, :], False, True)
+        act00 = silu("act00", u[0, 0][:])
+        turn(u[0, 1], prod0[:, 1, :], False, True)
+        act01 = silu("act01", u[0, 1][:])
+        turn(total0, act00, True, False)
+        turn(u[0, 2], prod0[:, 2, :], False, True)
+        act02 = silu("act02", u[0, 2][:])
+        turn(total0, act01, False, False)
+        turn(u[1, 0], prod10, False, True)
+        act10 = silu("act10", u[1, 0][:])
+        turn(total0, act02, False, True)
+        turn(u[1, 1], prod1[:, 0, :], False, True)
+        act11 = silu("act11", u[1, 1][:])
+        res0 = sbuf("res0", [P, V], F32)
+        nc.scalar.copy(res0[:], total0[:])
+        nc.sync.dma_start(out[0:P, :], res0[:])
+        nc.vector.tensor_tensor(prod1[:, 0, :], prod1[:, 1, :], sc[1][:], ADD)
+        total1 = psum.tile([P, V], F32, name="total1", tag="b4")
+        turn(total1, act10, True, False)
+        turn(total1, act11, False, True)
+        act12 = silu("act12", prod1[:, 0, :])
+        res1 = sbuf("res1", [P, V], F32)
+        nc.vector.tensor_tensor(res1[:], total1[:], act12[:], ADD)
         nc.sync.dma_start(out[P : 2 * P, :], res1[:])

@@ -70,8 +70,8 @@ def tile_picked_filmg_silu_p_kernel(
         nc.gpsimd.memset(xs[:].bitcast(I32), 0)
         xs_second = sbuf("xs_second", [P, S], U8)
         nc.gpsimd.memset(xs_second[:].bitcast(I32), 0)
-        offs_t = load_list("offs_t", offs)
         xw = [load_words(0)]
+        offs_t = load_list("offs_t", offs)
         for q in range(4):
             nc.sync.dma_start(xs[32 * q : 32 * q + 8, :].bitcast(I32), x_scales[:, 4 * q : 4 * q + 4, :].bitcast(I32))
         load_weight("g", w1, 0, BOTH)
@@ -100,8 +100,8 @@ def tile_picked_filmg_silu_p_kernel(
             raw, first = raws[name, z, blocks[0]]
             width = P * len(blocks)
             tile = sbuf("grp_%s%d%d" % (name, z, blocks[0]), [P, width, PACK], BF16)
-            dst = tile[:].rearrange("p (c i) t -> p c t i", i=4)
-            src = raw[:, :, first : first + width].rearrange("p t (c i) -> p c t i", i=4)
+            dst = tile[:].rearrange("p (c i) t -> p c t i", i=2)
+            src = raw[:, :, first : first + width].rearrange("p t (c i) -> p c t i", i=2)
             if on_vector:
                 nc.vector.tensor_copy(dst, src)
             else:
@@ -190,7 +190,11 @@ def tile_picked_filmg_silu_p_kernel(
         scaled(prod10[:], 1, 0)
         prod1 = sbuf("prod1", [P, 2, V], F32)
         scaled(prod1[:, 0, :], 1, 1)
-        scaled(prod1[:, 1, :], 1, 2)
+        for hv in range(HALVES):
+            cols = slice(hv * P, (hv + 1) * P)
+            nc.vector.tensor_tensor(
+                prod1[:, 1, cols], rows["h", 1][:].indirect(pos_t[2][:, 8 * hv : 8 * hv + 8]), gc[1][:, cols], MULT
+            )
 
         u = {}
         for b, d, tag in ((0, 0, "b0"), (0, 1, "b1"), (0, 2, "b2"), (1, 0, "b3"), (1, 1, "b6")):
@@ -213,11 +217,18 @@ def tile_picked_filmg_silu_p_kernel(
         res0 = sbuf("res0", [P, V], F32)
         nc.scalar.copy(res0[:], total0[:])
         nc.sync.dma_start(out[0:P, :], res0[:])
-        nc.vector.tensor_tensor(prod1[:, 0, :], prod1[:, 1, :], sc[1][:], ADD)
+        for hv in range(HALVES):
+            cols = slice(hv * P, (hv + 1) * P)
+            nc.vector.tensor_tensor(prod1[:, 0, cols], prod1[:, 1, cols], sc[1][:, cols], ADD)
         total1 = psum.tile([P, V], F32, name="total1", tag="b4")
         turn(total1, act10, True, False)
         turn(total1, act11, False, True)
-        act12 = silu("act12", prod1[:, 0, :])
+        act12 = sbuf("act12", [P, V], F32)
         res1 = sbuf("res1", [P, V], F32)
-        nc.vector.tensor_tensor(res1[:], total1[:], act12[:], ADD)
-        nc.sync.dma_start(out[P : 2 * P, :], res1[:])
+        for hv in range(HALVES):
+            cols = slice(hv * P, (hv + 1) * P)
+            nc.scalar.activation(act12[:, cols], prod1[:, 0, cols], SILU)
+        for hv in range(HALVES):
+            cols = slice(hv * P, (hv + 1) * P)
+            nc.vector.tensor_tensor(res1[:, cols], total1[:, cols], act12[:, cols], ADD)
+            nc.sync.dma_start(out[P : 2 * P, cols], res1[:, cols])

from contextlib import ExitStack

import concourse.mybir as mybir
from concourse.masks import make_identity

K, T, S, V, N = 1024, 2048, 512, 256, 256
FLOPS = 3 * 2 * K * N * S

F32 = mybir.dt.float32
BF16 = mybir.dt.bfloat16
I32 = mybir.dt.int32
U32 = mybir.dt.uint32
U16 = mybir.dt.uint16
U8 = mybir.dt.uint8
FP8X4 = mybir.dt.float8_e4m3fn_x4
FP4X4 = mybir.dt.float4_e2m1fn_x4
MULT = mybir.AluOpType.mult
ADD = mybir.AluOpType.add
SILU = mybir.ActivationFunctionType.Silu

P = 128
PACK = 4
K_PASS = P * PACK
PASSES = K // K_PASS
HALVES = V // P
BOTH = (0, 1)


def tile_picked_filmg_silu_p_kernel(
    tc, x_words, x_scales, w1, w2, w3, offs, cen, pos1, pos2, pos3, out
):
    nc = tc.nc
    with ExitStack() as ctx:
        keep = ctx.enter_context(tc.tile_pool(name="keep", bufs=1))
        psum = ctx.enter_context(tc.psum_pool(name="psum", bufs=1))

        def sbuf(name, shape, dtype, after=None):
            return keep.tile(shape, dtype, name=name, tag=after or name, align_bytes=64)

        def load_list(name, src):
            tile = keep.tile(list(src.shape), U16, name=name)
            nc.sync.dma_start(tile[:], src)
            return tile

        def load_words(z):
            tile = sbuf("xw%d" % z, [P, T], U16)
            nc.sync.dma_start(tile[:].bitcast(I32), x_words[z].bitcast(I32))
            return tile

        raws = {}

        def load_weight(name, w, z, blocks):
            raw = sbuf("raw_%s%d%d" % (name, z, blocks[0]), [P, PACK, P * len(blocks)], F32)
            rows_k = w[z * K_PASS : (z + 1) * K_PASS, blocks[0] * P : (blocks[-1] + 1) * P]
            nc.sync.dma_start(raw[:], rows_k.rearrange("(p j) n -> p j n", j=PACK))
            for i, b in enumerate(blocks):
                raws[name, z, b] = (raw, i * P)

        def gather(name, window, offsets, dtype, after=None):
            picked = sbuf(name, [P, 16 * offsets.shape[1]], dtype, after)
            nc.vector.tensor_copy(picked[:], window[:].indirect(offsets[:]))
            return picked

        warm_in = keep.tile([P, 1], F32, name="warm_in")
        nc.gpsimd.memset(warm_in[:], 0.0)
        warm_out = keep.tile([P, 1], F32, name="warm_out")
        nc.scalar.activation(warm_out[:], warm_in[:], SILU)

        xs = sbuf("xs", [P, T], U8)
        nc.gpsimd.memset(xs[:].bitcast(I32), 0)
        xs_second = sbuf("xs_second", [P, S], U8)
        nc.gpsimd.memset(xs_second[:].bitcast(I32), 0)
        xw = [load_words(0)]
        offs_t = load_list("offs_t", offs)
        for q in range(4):
            nc.sync.dma_start(xs[32 * q : 32 * q + 8, :].bitcast(I32), x_scales[:, 4 * q : 4 * q + 4, :].bitcast(I32))
        load_weight("g", w1, 0, BOTH)
        xw.append(load_words(1))
        load_weight("g", w1, 1, BOTH)
        load_weight("s", w2, 0, BOTH)
        xg = [gather("xg0", xw[0], offs_t, U16)]
        xs_first = gather("xs_first", xs, offs_t, U8)
        nc.sync.dma_start(xs_second[0:112, :].bitcast(I32), xs_first[4:116, :].bitcast(I32))
        xsg = [xs_first, xs_second]
        cen_t = load_list("cen_t", cen)
        load_weight("s", w2, 1, BOTH)
        load_weight("h", w3, 0, (0,))
        load_weight("h", w3, 1, (0,))
        load_weight("h", w3, 0, (1,))
        load_weight("h", w3, 1, (1,))
        pos_t = [load_list("pos1_t", pos1), load_list("pos2_t", pos2), load_list("pos3_t", pos3)]

        ident = keep.tile([P, P], F32, name="ident")
        make_identity(nc, ident[:])

        banks, rows, grouped = {}, {}, {}
        bank_tag = {("g", 0): "b0", ("g", 1): "b1", ("s", 0): "b2", ("s", 1): "b3", ("h", 0): "b4", ("h", 1): "b5"}

        def cast(name, z, blocks, on_vector=False):
            raw, first = raws[name, z, blocks[0]]
            width = P * len(blocks)
            tile = sbuf("grp_%s%d%d" % (name, z, blocks[0]), [P, width, PACK], BF16)
            dst = tile[:].rearrange("p (c i) t -> p c t i", i=2)
            src = raw[:, :, first : first + width].rearrange("p t (c i) -> p c t i", i=2)
            if on_vector:
                nc.vector.tensor_copy(dst, src)
            else:
                nc.scalar.copy(dst, src)
            grouped[name, z, blocks[0]] = tile

        def multiply(name, z, blocks):
            label = "%s%d%d" % (name, z, blocks[0])
            width = P * len(blocks)
            codes = sbuf("codes_" + label, [P, width], U32)
            plane = sbuf("plane_" + label, [P, width], U8)
            nc.vector.quantize_mx(
                out=codes[:].bitcast(FP8X4),
                scales=plane[:],
                in_=grouped[name, z, blocks[0]][:].rearrange("p n t -> p (n t)"),
            )
            for i, b in enumerate(blocks):
                if z == 0:
                    banks[name, b] = psum.tile([P, S], F32, name="acc_%s%d" % (name, b), tag=bank_tag[name, b])
                cols = slice(i * P, (i + 1) * P)
                nc.tensor.matmul_mx(
                    out=banks[name, b][:],
                    lhsT=codes[:, cols].bitcast(FP8X4),
                    lhsT_scale=plane[:, cols],
                    rhs=xg[z][:].bitcast(FP4X4),
                    rhs_scale=xsg[z][:],
                    start=(z == 0),
                    stop=(z == PASSES - 1),
                )

        def leave(name, b, after=None):
            rows[name, b] = sbuf("row_%s%d" % (name, b), [P, S], F32, after)
            nc.scalar.copy(rows[name, b][:], banks[name, b][:])

        def scaled(dst, b, d):
            nc.vector.tensor_tensor(dst, rows["h", b][:].indirect(pos_t[d][:]), gc[b][:], MULT)

        def turn(bank, src, start, stop):
            for hv in range(HALVES):
                cols = slice(hv * P, (hv + 1) * P)
                nc.tensor.matmul(
                    bank[:, cols], src[:, cols], ident[:], is_transpose=True,
                    start=(start and hv == 0), stop=(stop and hv == HALVES - 1),
                )

        def silu(name, src):
            act = sbuf(name, [P, V], F32)
            nc.scalar.activation(act[:], src, SILU)
            return act

        cast("g", 0, BOTH)
        multiply("g", 0, BOTH)
        xg.append(gather("xg1", xw[1], offs_t, U16, "grp_g00"))
        cast("g", 1, (0,))
        cast("g", 1, (1,))
        multiply("g", 1, (0,))
        multiply("g", 1, (1,))
        cast("s", 0, BOTH, True)
        leave("g", 0)
        multiply("s", 0, BOTH)
        cast("s", 1, (0,))
        cast("s", 1, (1,))
        gc = [gather("gc0", rows["g", 0], cen_t, F32)]
        cast("h", 0, (0,), True)
        multiply("s", 1, (0,))
        multiply("h", 0, (0,))
        cast("h", 1, (0,), True)
        multiply("h", 1, (0,))
        multiply("s", 1, (1,))
        leave("g", 1, "raw_s10")
        leave("s", 0)
        gc.append(gather("gc1", rows["g", 1], cen_t, F32, "grp_h10"))
        cast("h", 0, (1,), True)
        cast("h", 1, (1,))
        leave("s", 1)
        leave("h", 0)
        sc = [gather("sc0", rows["s", 0], cen_t, F32)]
        multiply("h", 0, (1,))
        multiply("h", 1, (1,))
        sc.append(gather("sc1", rows["s", 1], cen_t, F32))
        prod0 = sbuf("prod0", [P, 3, V], F32, "row_s1")
        for d in range(3):
            scaled(prod0[:, d, :], 0, d)
        leave("h", 1)
        prod10 = sbuf("prod10", [P, V], F32)
        scaled(prod10[:], 1, 0)
        prod1 = sbuf("prod1", [P, 2, V], F32)
        scaled(prod1[:, 0, :], 1, 1)
        for hv in range(HALVES):
            cols = slice(hv * P, (hv + 1) * P)
            nc.vector.tensor_tensor(
                prod1[:, 1, cols], rows["h", 1][:].indirect(pos_t[2][:, 8 * hv : 8 * hv + 8]), gc[1][:, cols], MULT
            )

        u = {}
        for b, d, tag in ((0, 0, "b0"), (0, 1, "b1"), (0, 2, "b2"), (1, 0, "b3"), (1, 1, "b6")):
            u[b, d] = psum.tile([P, V], F32, name="u%d%d" % (b, d), tag=tag)
            turn(u[b, d], sc[b], True, False)
        total0 = psum.tile([P, V], F32, name="total0", tag="b7")
        turn(u[0, 0], prod0[:, 0, :], False, True)
        act00 = silu("act00", u[0, 0][:])
        turn(u[0, 1], prod0[:, 1, :], False, True)
        act01 = silu("act01", u[0, 1][:])
        turn(total0, act00, True, False)
        turn(u[0, 2], prod0[:, 2, :], False, True)
        act02 = silu("act02", u[0, 2][:])
        turn(total0, act01, False, False)
        turn(u[1, 0], prod10, False, True)
        act10 = silu("act10", u[1, 0][:])
        turn(total0, act02, False, True)
        turn(u[1, 1], prod1[:, 0, :], False, True)
        act11 = silu("act11", u[1, 1][:])
        res0 = sbuf("res0", [P, V], F32)
        nc.scalar.copy(res0[:], total0[:])
        nc.sync.dma_start(out[0:P, :], res0[:])
        for hv in range(HALVES):
            cols = slice(hv * P, (hv + 1) * P)
            nc.vector.tensor_tensor(prod1[:, 0, cols], prod1[:, 1, cols], sc[1][:, cols], ADD)
        total1 = psum.tile([P, V], F32, name="total1", tag="b4")
        turn(total1, act10, True, False)
        turn(total1, act11, False, True)
        act12 = sbuf("act12", [P, V], F32)
        res1 = sbuf("res1", [P, V], F32)
        for hv in range(HALVES):
            cols = slice(hv * P, (hv + 1) * P)
            nc.scalar.activation(act12[:, cols], prod1[:, 0, cols], SILU)
        for hv in range(HALVES):
            cols = slice(hv * P, (hv + 1) * P)
            nc.vector.tensor_tensor(res1[:, cols], total1[:, cols], act12[:, cols], ADD)
            nc.sync.dma_start(out[P : 2 * P, cols], res1[:, cols])
